import numpy as np
import ml_dtypes


def mxq(x, axis, fmt="e4m3"):
    dtype, down = {"e4m3": (ml_dtypes.float8_e4m3fn, 7), "e5m2": (ml_dtypes.float8_e5m2, 14)}[fmt]
    v = np.moveaxis(np.asarray(x, np.float32).astype(ml_dtypes.bfloat16).astype(np.float64), axis, -1)
    blocks = v.reshape(v.shape[:-1] + (-1, 32))
    amax = np.abs(blocks).max(-1, keepdims=True)
    byte = np.maximum(np.where(amax > 0, np.frexp(amax)[1] - 1 + 127, 0) - down, 1)
    scale = np.exp2(byte - 127.0)
    codes = (blocks / scale).astype(np.float32).astype(dtype).astype(np.float64)
    return np.moveaxis((codes * scale).reshape(v.shape), -1, axis)


WIDE = False


def mx_kscale(k):
    if not WIDE:
        return np.ones(k)
    levels = np.array([30, -30])
    if k % 512:
        return np.exp2(np.random.permutation(np.resize(levels, k // 32))).repeat(32)
    a = np.empty((k // 512, 16))
    for p in range(k // 512):
        a[p, :8] = np.random.permutation(np.resize(levels, 8))
        for g in range(8):
            far = levels[np.abs(levels - a[p, g]) >= 10]
            a[p, g + 8] = far[np.random.randint(len(far))]
    return np.exp2(a.ravel()).repeat(32)


def f64(x):
    return np.asarray(x).astype(np.float64)


def striped(idx):
    return np.tile(np.asarray(idx).reshape(-1, 16).T, (8, 1)).astype(np.uint16)


def unstriped(offs):
    return offs[:16].T.reshape(-1).astype(np.int64)


E2M1 = np.array([0.0, 0.5, 1.0, 1.5, 2.0, 3.0, 4.0, 6.0, -0.0, -0.5, -1.0, -1.5, -2.0, -3.0, -4.0, -6.0])


def pack_weight(w, fmt):
    k, n = w.shape
    w = f64(np.asarray(w, np.float32).astype(ml_dtypes.bfloat16)).reshape(k // 32, 32, n)
    amax = np.abs(w).max(1)
    if fmt in ("e4m3", "e5m2"):
        byte = np.frexp(amax)[1] - 1 + 127 - (7 if fmt == "e4m3" else 14)
    else:
        mant, ex = np.frexp(amax / 6.0)
        byte = np.where(mant > 0.5, ex, ex - 1) + 127
    byte = np.clip(np.where(amax > 0, byte, 1), 1, 254)
    scaled = (w * np.exp2(127.0 - byte)[:, None, :]).reshape(k, n).astype(np.float32)
    by_word = np.ascontiguousarray(scaled.reshape(k // 512, 128, 4, n).transpose(0, 1, 3, 2))
    if fmt in ("e4m3", "e5m2"):
        words = by_word.astype(ml_dtypes.float8_e4m3fn if fmt == "e4m3" else ml_dtypes.float8_e5m2).view(np.uint8)
    else:
        c = by_word.astype(ml_dtypes.float4_e2m1fn).view(np.uint8) & 0xF
        words = (c[..., 0::2] | (c[..., 1::2] << 4)).reshape(k // 512, 128, 2 * n)
    return np.ascontiguousarray(words), np.ascontiguousarray(byte.astype(np.uint8).reshape(k // 512, 16, n))


def unpack_weight(words, scales, fmt):
    g, _, n = scales.shape
    words = np.ascontiguousarray(words).reshape(g, 128, n, -1)
    if fmt in ("e4m3", "e5m2"):
        vals = words.view(ml_dtypes.float8_e4m3fn if fmt == "e4m3" else ml_dtypes.float8_e5m2).astype(np.float64)
    else:
        nib = np.empty((g, 128, n, 4), np.uint8)
        nib[..., 0::2] = words & 0xF
        nib[..., 1::2] = words >> 4
        vals = E2M1[nib]
    vals = vals * np.repeat(np.exp2(scales.astype(np.float64) - 127.0), 8, axis=1)[..., None]
    return vals.transpose(0, 1, 3, 2).reshape(g * 512, n)


K, T, J, N, S, L = 1024, 1024, 256, 256, 512, 512


def setup_inputs():
    n = np.random.standard_normal
    idx = np.random.permutation(T)[:J]
    idx2 = np.random.permutation(S)[:J]
    fk = mx_kscale(K)
    fl = mx_kscale(L)
    xtp = pack_weight(n((K, T)) * np.random.uniform(0.4, 1.6, (1, T)) / fk[:, None], "e5m2")
    wap = pack_weight(n((K, N)) * 1 / np.sqrt(K) * fk[:, None], "e5m2")
    wbp = pack_weight(n((L, N)) * 1 / np.sqrt(L) * fl[:, None], "e4m3")
    return {
        "xt_words": xtp[0],
        "xt_scales": xtp[1],
        "wa_words": wap[0],
        "wa_scales": wap[1],
        "xs": (n((L, S)) * np.random.uniform(0.4, 1.6, (1, S)) / fl[:, None]).astype(np.float32),
        "wb_words": wbp[0],
        "wb_scales": wbp[1],
        "bi": (np.random.uniform(-0.6, 0.6, (1, N))).astype(np.float32),
        "offs": striped(idx),
        "offs2": striped(idx2),
    }


def reference(xt_words, xt_scales, wa_words, wa_scales, xs, wb_words, wb_scales, bi, offs, offs2):
    idx = unstriped(offs)
    idx2 = unstriped(offs2)
    xtu = unpack_weight(xt_words, xt_scales, "e5m2")
    wau = unpack_weight(wa_words, wa_scales, "e5m2")
    wbu = unpack_weight(wb_words, wb_scales, "e4m3")
    xtidxg = xtu[:, idx]
    a = xtidxg.T @ wau
    xsidx2q = mxq(f64(xs)[:, idx2], 0, "e5m2")
    b0 = xsidx2q.T @ wbu
    b2 = b0 + f64(bi)
    sm = np.minimum(a, b2)
    y = np.maximum(a, b2) - 2.0 * np.mean(sm, axis=1, keepdims=True)
    return y

@@ -1,0 +1,130 @@
+from contextlib import ExitStack
+
+import concourse.mybir as mybir
+from concourse.masks import make_identity
+
+K, T, J, N, S, L = 1024, 1024, 256, 256, 512, 512
+FLOPS = 2 * J * N * (K + L)
+
+F32 = mybir.dt.float32
+BF16 = mybir.dt.bfloat16
+I32 = mybir.dt.int32
+U32 = mybir.dt.uint32
+U16 = mybir.dt.uint16
+U8 = mybir.dt.uint8
+E5 = mybir.dt.float8_e5m2_x4
+E4 = mybir.dt.float8_e4m3fn_x4
+ALU = mybir.AluOpType
+ACT = mybir.ActivationFunctionType
+P = 128
+PASSES = K // 512
+JT = J // P
+
+
+def tile_list_rows_othertable_largerlesssmaller_kernel(
+    tc, xt_words, xt_scales, wa_words, wa_scales, xs, wb_words, wb_scales, bi, offs, offs2, out
+):
+    nc = tc.nc
+    with ExitStack() as ctx:
+        sb = ctx.enter_context(tc.tile_pool(name="sb", bufs=1))
+        ps = ctx.enter_context(tc.psum_pool(name="ps", bufs=1))
+
+        list_t = sb.tile([P, J // 16], U16, name="list_t")
+        list_s = sb.tile([P, J // 16], U16, name="list_s")
+        xs_sb = [sb.tile([P, 2, S], F32, name="xs_sb%d" % h) for h in range(2)]
+        xt_w = [sb.tile([P, T], U32, name="xt_w%d" % z) for z in range(PASSES)]
+        xt_s = sb.tile([P, PASSES, T], U8, name="xt_s")
+        wa_w = sb.tile([P, PASSES, N], U32, name="wa_w", align_bytes=64)
+        wa_s = sb.tile([P, PASSES, N], U8, name="wa_s", align_bytes=64)
+        wb_w = sb.tile([P, N], U32, name="wb_w", align_bytes=64)
+        wb_s = sb.tile([P, N], U8, name="wb_s", align_bytes=64)
+        bi_col = sb.tile([P, 2], F32, name="bi_col")
+        ident = sb.tile([P, P], F32, name="ident")
+
+        nc.vector.memset(xt_s[:, 0, :].bitcast(I32), 0)
+        nc.gpsimd.memset(xt_s[:, 1, :].bitcast(I32), 0)
+        nc.vector.memset(wb_s[:].bitcast(I32), 0)
+        nc.vector.memset(wa_s[:].bitcast(I32), 0)
+
+        xs_rows = xs.rearrange("(p t) s -> p t s", t=4)
+        xt_s_rows = xt_scales.rearrange("z q c -> q z c").bitcast(I32)
+        wa_s_rows = wa_scales.rearrange("z q c -> q z c").bitcast(I32)
+        wb_s_rows = wb_scales[0].bitcast(I32)
+        nc.gpsimd.dma_start(bi_col[:], bi.rearrange("o (p c) -> p (o c)", c=2))
+        make_identity(nc, ident[:])
+        nc.sync.dma_start(list_s[:], offs2)
+        nc.sync.dma_start(xs_sb[0][:], xs_rows[:, 0:2, :])
+        nc.sync.dma_start(list_t[:], offs)
+        for q in range(4):
+            nc.sync.dma_start(xt_s[32 * q : 32 * q + 4].bitcast(I32), xt_s_rows[4 * q : 4 * q + 4])
+        nc.sync.dma_start(xs_sb[1][:], xs_rows[:, 2:4, :])
+        nc.sync.dma_start(xt_w[0][:].bitcast(I32), xt_words[0].rearrange("p c r -> p (c r)").bitcast(I32))
+        nc.sync.dma_start(wb_w[:].bitcast(I32), wb_words[0].rearrange("p c r -> p (c r)").bitcast(I32))
+        for q in range(4):
+            nc.sync.dma_start(wb_s[32 * q : 32 * q + 4].bitcast(I32), wb_s_rows[4 * q : 4 * q + 4])
+        nc.sync.dma_start(xt_w[1][:].bitcast(I32), xt_words[1].rearrange("p c r -> p (c r)").bitcast(I32))
+        nc.sync.dma_start(wa_w[:].bitcast(I32), wa_words.rearrange("z p c r -> p z (c r)").bitcast(I32))
+        for q in range(4):
+            nc.sync.dma_start(wa_s[32 * q : 32 * q + 4].bitcast(I32), wa_s_rows[4 * q : 4 * q + 4])
+
+        g_s = [sb.tile([P, J], U8, name="g_s%d" % z, align_bytes=64) for z in range(PASSES)]
+        g_w = [sb.tile([P, J], U32, name="g_w%d" % z, align_bytes=64) for z in range(PASSES)]
+        for z in range(PASSES):
+            nc.vector.tensor_copy(g_s[z][:], xt_s[:, z, :].indirect(list_t[:]))
+
+        xs_g = sb.tile([P, 4, J], F32, name="xs_g")
+        for t in range(4):
+            win = xs_sb[t // 2][:, t % 2, :].indirect(list_s[:])
+            if t < 3:
+                nc.scalar.activation(xs_g[:, t, :], win, ACT.Copy)
+            else:
+                nc.vector.tensor_copy(xs_g[:, t, :], win)
+
+        bi_ps = ps.tile([P, 2, P], F32, name="bi_ps")
+        for c in range(2):
+            nc.tensor.transpose(bi_ps[:, c, :], bi_col[:, c : c + 1].to_broadcast([P, P]), ident[:])
+        bi_all = sb.tile([P, N], F32, name="bi_all")
+        nc.scalar.copy(bi_all[:].rearrange("q (p c) -> q p c", c=2), bi_ps[:].rearrange("q c p -> q p c"))
+
+        woven = [sb.tile([P, P, 4], BF16, name="woven%d" % h, align_bytes=64) for h in range(JT)]
+        q_w = [sb.tile([P, P], U32, name="q_w%d" % h, align_bytes=64) for h in range(JT)]
+        q_s = [sb.tile([P, P], U8, name="q_s%d" % h, align_bytes=64) for h in range(JT)]
+        for h in range(JT):
+            nc.vector.tensor_copy(
+                woven[h][:].rearrange("p (c i) t -> p c t i", i=4),
+                xs_g[:, :, h * P : (h + 1) * P].rearrange("p t (c i) -> p c t i", i=4),
+            )
+        for h in range(JT):
+            nc.vector.quantize_mx(
+                out=q_w[h][:].bitcast(E5), scales=q_s[h][:], in_=woven[h][:].rearrange("p c t -> p (c t)")
+            )
+        nc.vector.tensor_copy(g_w[0][:], xt_w[0][:].indirect(list_t[:]))
+        b2 = [sb.tile([P, N], F32, name="b2_%d" % h) for h in range(JT)]
+        for h in range(JT):
+            b_ps = ps.tile([P, N], F32, name="b_ps%d" % h)
+            nc.tensor.matmul_mx(
+                out=b_ps[:], lhsT=q_w[h][:].bitcast(E5), lhsT_scale=q_s[h][:],
+                rhs=wb_w[:].bitcast(E4), rhs_scale=wb_s[:], start=True, stop=True,
+            )
+            nc.vector.tensor_tensor(b2[h][:], b_ps[:], bi_all[:], ALU.add)
+        nc.vector.tensor_copy(g_w[1][:], xt_w[1][:].indirect(list_t[:]))
+
+        for h in range(JT):
+            cols = slice(h * P, (h + 1) * P)
+            a_ps = ps.tile([P, N], F32, name="a_ps%d" % h)
+            for z in range(PASSES):
+                nc.tensor.matmul_mx(
+                    out=a_ps[:], lhsT=g_w[z][:, cols].bitcast(E5), lhsT_scale=g_s[z][:, cols],
+                    rhs=wa_w[:, z, :].bitcast(E5), rhs_scale=wa_s[:, z, :],
+                    start=(z == 0), stop=(z == PASSES - 1),
+                )
+            sm = sb.tile([P, N], F32, name="sm%d" % h)
+            sm_sum = sb.tile([P, 1], F32, name="sm_sum%d" % h)
+            shift = sb.tile([P, 1], F32, name="shift%d" % h)
+            mx = sb.tile([P, N], F32, name="mx%d" % h)
+            y = sb.tile([P, N], F32, name="y%d" % h)
+            nc.vector.scalar_tensor_tensor(sm[:], a_ps[:], 1.0, b2[h][:], ALU.mult, ALU.min, accum_out=sm_sum[:])
+            nc.vector.tensor_tensor(mx[:], a_ps[:], b2[h][:], ALU.max)
+            nc.scalar.activation(shift[:], sm_sum[:], ACT.Copy, scale=-2.0 / N)
+            nc.scalar.activation(y[:], mx[:], ACT.Identity, bias=shift[:])
+            (nc.sync if h == 0 else nc.scalar).dma_start(out[cols, :], y[:])

@@ -34,15 +34,19 @@ def tile_list_rows_othertable_largerlesssmaller_kernel(
         xs_sb = [sb.tile([P, 2, S], F32, name="xs_sb%d" % h) for h in range(2)]
         xt_w = [sb.tile([P, T], U32, name="xt_w%d" % z) for z in range(PASSES)]
         xt_s = sb.tile([P, PASSES, T], U8, name="xt_s")
-        wa_w = sb.tile([P, PASSES, N], U32, name="wa_w", align_bytes=64)
+        wa_w = [sb.tile([P, N], U32, name="wa_w%d" % z, align_bytes=64) for z in range(PASSES)]
         wa_s = sb.tile([P, PASSES, N], U8, name="wa_s", align_bytes=64)
         wb_w = sb.tile([P, N], U32, name="wb_w", align_bytes=64)
         wb_s = sb.tile([P, N], U8, name="wb_s", align_bytes=64)
         bi_col = sb.tile([P, 2], F32, name="bi_col")
         ident = sb.tile([P, P], F32, name="ident")
 
+        warm = sb.tile([P, 2], F32, name="warm")
         nc.vector.memset(xt_s[:, 0, :].bitcast(I32), 0)
+        nc.vector.memset(ident[:], 0.0)
         nc.gpsimd.memset(xt_s[:, 1, :].bitcast(I32), 0)
+        nc.vector.memset(warm[:, 0:1], 0.0)
+        nc.scalar.activation(warm[:, 1:2], warm[:, 0:1], ACT.Copy)
         nc.vector.memset(wb_s[:].bitcast(I32), 0)
         nc.vector.memset(wa_s[:].bitcast(I32), 0)
 
@@ -50,11 +54,13 @@ def tile_list_rows_othertable_largerlesssmaller_kernel(
         xt_s_rows = xt_scales.rearrange("z q c -> q z c").bitcast(I32)
         wa_s_rows = wa_scales.rearrange("z q c -> q z c").bitcast(I32)
         wb_s_rows = wb_scales[0].bitcast(I32)
+        make_identity(nc, ident[:], nomemset=True)
         nc.gpsimd.dma_start(bi_col[:], bi.rearrange("o (p c) -> p (o c)", c=2))
-        make_identity(nc, ident[:])
+        for q in range(4):
+            nc.gpsimd.dma_start(wa_s[32 * q : 32 * q + 4].bitcast(I32), wa_s_rows[4 * q : 4 * q + 4])
         nc.sync.dma_start(list_s[:], offs2)
-        nc.sync.dma_start(xs_sb[0][:], xs_rows[:, 0:2, :])
         nc.sync.dma_start(list_t[:], offs)
+        nc.sync.dma_start(xs_sb[0][:], xs_rows[:, 0:2, :])
         for q in range(4):
             nc.sync.dma_start(xt_s[32 * q : 32 * q + 4].bitcast(I32), xt_s_rows[4 * q : 4 * q + 4])
         nc.sync.dma_start(xs_sb[1][:], xs_rows[:, 2:4, :])
@@ -63,9 +69,8 @@ def tile_list_rows_othertable_largerlesssmaller_kernel(
         for q in range(4):
             nc.sync.dma_start(wb_s[32 * q : 32 * q + 4].bitcast(I32), wb_s_rows[4 * q : 4 * q + 4])
         nc.sync.dma_start(xt_w[1][:].bitcast(I32), xt_words[1].rearrange("p c r -> p (c r)").bitcast(I32))
-        nc.sync.dma_start(wa_w[:].bitcast(I32), wa_words.rearrange("z p c r -> p z (c r)").bitcast(I32))
-        for q in range(4):
-            nc.sync.dma_start(wa_s[32 * q : 32 * q + 4].bitcast(I32), wa_s_rows[4 * q : 4 * q + 4])
+        nc.sync.dma_start(wa_w[0][:].bitcast(I32), wa_words[0].rearrange("p c r -> p (c r)").bitcast(I32))
+        nc.sync.dma_start(wa_w[1][:].bitcast(I32), wa_words[1].rearrange("p c r -> p (c r)").bitcast(I32))
 
         g_s = [sb.tile([P, J], U8, name="g_s%d" % z, align_bytes=64) for z in range(PASSES)]
         g_w = [sb.tile([P, J], U32, name="g_w%d" % z, align_bytes=64) for z in range(PASSES)]
@@ -73,12 +78,13 @@ def tile_list_rows_othertable_largerlesssmaller_kernel(
             nc.vector.tensor_copy(g_s[z][:], xt_s[:, z, :].indirect(list_t[:]))
 
         xs_g = sb.tile([P, 4, J], F32, name="xs_g")
-        for t in range(4):
-            win = xs_sb[t // 2][:, t % 2, :].indirect(list_s[:])
-            if t < 3:
-                nc.scalar.activation(xs_g[:, t, :], win, ACT.Copy)
-            else:
-                nc.vector.tensor_copy(xs_g[:, t, :], win)
+        for t in range(2):
+            nc.scalar.activation(xs_g[:, t, :], xs_sb[0][:, t, :].indirect(list_s[:]), ACT.Copy)
+        for t, h in ((2, 0), (2, 1), (3, 1)):
+            nc.scalar.activation(
+                xs_g[:, t, h * P : (h + 1) * P], xs_sb[1][:, t - 2, :].indirect(list_s[:, 8 * h : 8 * h + 8]), ACT.Copy
+            )
+        nc.vector.tensor_copy(xs_g[:, 3, 0:P], xs_sb[1][:, 1, :].indirect(list_s[:, 0:8]))
 
         bi_ps = ps.tile([P, 2, P], F32, name="bi_ps")
         for c in range(2):
@@ -90,7 +96,7 @@ def tile_list_rows_othertable_largerlesssmaller_kernel(
         q_w = [sb.tile([P, P], U32, name="q_w%d" % h, align_bytes=64) for h in range(JT)]
         q_s = [sb.tile([P, P], U8, name="q_s%d" % h, align_bytes=64) for h in range(JT)]
         for h in range(JT):
-            nc.vector.tensor_copy(
+            (nc.vector.tensor_copy if h == 0 else nc.scalar.copy)(
                 woven[h][:].rearrange("p (c i) t -> p c t i", i=4),
                 xs_g[:, :, h * P : (h + 1) * P].rearrange("p t (c i) -> p c t i", i=4),
             )
@@ -115,7 +121,7 @@ def tile_list_rows_othertable_largerlesssmaller_kernel(
             for z in range(PASSES):
                 nc.tensor.matmul_mx(
                     out=a_ps[:], lhsT=g_w[z][:, cols].bitcast(E5), lhsT_scale=g_s[z][:, cols],
-                    rhs=wa_w[:, z, :].bitcast(E5), rhs_scale=wa_s[:, z, :],
+                    rhs=wa_w[z][:].bitcast(E5), rhs_scale=wa_s[:, z, :],
                     start=(z == 0), stop=(z == PASSES - 1),
                 )
             sm = sb.tile([P, N], F32, name="sm%d" % h)
@@ -126,5 +132,8 @@ def tile_list_rows_othertable_largerlesssmaller_kernel(
             nc.vector.scalar_tensor_tensor(sm[:], a_ps[:], 1.0, b2[h][:], ALU.mult, ALU.min, accum_out=sm_sum[:])
             nc.vector.tensor_tensor(mx[:], a_ps[:], b2[h][:], ALU.max)
             nc.scalar.activation(shift[:], sm_sum[:], ACT.Copy, scale=-2.0 / N)
-            nc.scalar.activation(y[:], mx[:], ACT.Identity, bias=shift[:])
+            if h == 0:
+                nc.scalar.activation(y[:], mx[:], ACT.Identity, bias=shift[:])
+            else:
+                nc.vector.tensor_scalar(y[:], mx[:], shift[:], None, ALU.add)
             (nc.sync if h == 0 else nc.scalar).dma_start(out[cols, :], y[:])

@@ -19,6 +19,7 @@ ACT = mybir.ActivationFunctionType
 P = 128
 PASSES = K // 512
 JT = J // P
+SC = -2.0 / N
 
 
 def tile_list_rows_othertable_largerlesssmaller_kernel(
@@ -31,10 +32,10 @@ def tile_list_rows_othertable_largerlesssmaller_kernel(
 
         list_t = sb.tile([P, J // 16], U16, name="list_t")
         list_s = sb.tile([P, J // 16], U16, name="list_s")
-        xs_sb = [sb.tile([P, 2, S], F32, name="xs_sb%d" % h) for h in range(2)]
-        xt_w = [sb.tile([P, T], U32, name="xt_w%d" % z) for z in range(PASSES)]
+        xs_sb = [sb.tile([P, 2, S], F32, name="xs_sb%d" % h, tag="xs_sb%d" % h) for h in range(2)]
+        xt_w = [sb.tile([P, T], U32, name="xt_w%d" % z, tag="xt_w%d" % z) for z in range(PASSES)]
         xt_s = sb.tile([P, PASSES, T], U8, name="xt_s")
-        wa_w = [sb.tile([P, N], U32, name="wa_w%d" % z, align_bytes=64) for z in range(PASSES)]
+        wa_w = sb.tile([P, PASSES, N], U32, name="wa_w", align_bytes=64)
         wa_s = sb.tile([P, PASSES, N], U8, name="wa_s", align_bytes=64)
         wb_w = sb.tile([P, N], U32, name="wb_w", align_bytes=64)
         wb_s = sb.tile([P, N], U8, name="wb_s", align_bytes=64)
@@ -43,7 +44,6 @@ def tile_list_rows_othertable_largerlesssmaller_kernel(
 
         warm = sb.tile([P, 2], F32, name="warm")
         nc.vector.memset(xt_s[:, 0, :].bitcast(I32), 0)
-        nc.vector.memset(ident[:], 0.0)
         nc.gpsimd.memset(xt_s[:, 1, :].bitcast(I32), 0)
         nc.vector.memset(warm[:, 0:1], 0.0)
         nc.scalar.activation(warm[:, 1:2], warm[:, 0:1], ACT.Copy)
@@ -54,10 +54,8 @@ def tile_list_rows_othertable_largerlesssmaller_kernel(
         xt_s_rows = xt_scales.rearrange("z q c -> q z c").bitcast(I32)
         wa_s_rows = wa_scales.rearrange("z q c -> q z c").bitcast(I32)
         wb_s_rows = wb_scales[0].bitcast(I32)
-        make_identity(nc, ident[:], nomemset=True)
         nc.gpsimd.dma_start(bi_col[:], bi.rearrange("o (p c) -> p (o c)", c=2))
-        for q in range(4):
-            nc.gpsimd.dma_start(wa_s[32 * q : 32 * q + 4].bitcast(I32), wa_s_rows[4 * q : 4 * q + 4])
+        make_identity(nc, ident[:])
         nc.sync.dma_start(list_s[:], offs2)
         nc.sync.dma_start(list_t[:], offs)
         nc.sync.dma_start(xs_sb[0][:], xs_rows[:, 0:2, :])
@@ -69,51 +67,53 @@ def tile_list_rows_othertable_largerlesssmaller_kernel(
         for q in range(4):
             nc.sync.dma_start(wb_s[32 * q : 32 * q + 4].bitcast(I32), wb_s_rows[4 * q : 4 * q + 4])
         nc.sync.dma_start(xt_w[1][:].bitcast(I32), xt_words[1].rearrange("p c r -> p (c r)").bitcast(I32))
-        nc.sync.dma_start(wa_w[0][:].bitcast(I32), wa_words[0].rearrange("p c r -> p (c r)").bitcast(I32))
-        nc.sync.dma_start(wa_w[1][:].bitcast(I32), wa_words[1].rearrange("p c r -> p (c r)").bitcast(I32))
+        nc.sync.dma_start(wa_w[:].bitcast(I32), wa_words.rearrange("z p c r -> p z (c r)").bitcast(I32))
+        for q in range(4):
+            nc.sync.dma_start(wa_s[32 * q : 32 * q + 4].bitcast(I32), wa_s_rows[4 * q : 4 * q + 4])
 
         g_s = [sb.tile([P, J], U8, name="g_s%d" % z, align_bytes=64) for z in range(PASSES)]
-        g_w = [sb.tile([P, J], U32, name="g_w%d" % z, align_bytes=64) for z in range(PASSES)]
         for z in range(PASSES):
             nc.vector.tensor_copy(g_s[z][:], xt_s[:, z, :].indirect(list_t[:]))
 
-        xs_g = sb.tile([P, 4, J], F32, name="xs_g")
-        for t in range(2):
-            nc.scalar.activation(xs_g[:, t, :], xs_sb[0][:, t, :].indirect(list_s[:]), ACT.Copy)
-        for t, h in ((2, 0), (2, 1), (3, 1)):
-            nc.scalar.activation(
-                xs_g[:, t, h * P : (h + 1) * P], xs_sb[1][:, t - 2, :].indirect(list_s[:, 8 * h : 8 * h + 8]), ACT.Copy
-            )
-        nc.vector.tensor_copy(xs_g[:, 3, 0:P], xs_sb[1][:, 1, :].indirect(list_s[:, 0:8]))
+        xs_g = [sb.tile([P, 4, P], F32, name="xs_g%d" % h) for h in range(JT)]
+        for t, h in ((0, 0), (1, 0), (0, 1), (1, 1), (2, 0), (3, 0), (2, 1), (3, 1)):
+            win = xs_sb[t // 2][:, t % 2, :].indirect(list_s[:, 8 * h : 8 * h + 8])
+            if (t, h) == (3, 0):
+                nc.vector.tensor_copy(xs_g[h][:, t, :], win)
+            else:
+                nc.scalar.activation(xs_g[h][:, t, :], win, ACT.Copy)
 
         bi_ps = ps.tile([P, 2, P], F32, name="bi_ps")
         for c in range(2):
             nc.tensor.transpose(bi_ps[:, c, :], bi_col[:, c : c + 1].to_broadcast([P, P]), ident[:])
-        bi_all = sb.tile([P, N], F32, name="bi_all")
-        nc.scalar.copy(bi_all[:].rearrange("q (p c) -> q p c", c=2), bi_ps[:].rearrange("q c p -> q p c"))
+        bi_all = sb.tile([P, N], F32, name="bi_all", tag="xs_sb1")
+        nc.scalar.activation(
+            bi_all[:].rearrange("q (p c) -> q p c", c=2), bi_ps[:].rearrange("q c p -> q p c"), ACT.Copy, scale=SC
+        )
 
-        woven = [sb.tile([P, P, 4], BF16, name="woven%d" % h, align_bytes=64) for h in range(JT)]
+        woven = [sb.tile([P, P, 4], BF16, name="woven%d" % h, tag="woven%d" % h, align_bytes=64) for h in range(JT)]
         q_w = [sb.tile([P, P], U32, name="q_w%d" % h, align_bytes=64) for h in range(JT)]
         q_s = [sb.tile([P, P], U8, name="q_s%d" % h, align_bytes=64) for h in range(JT)]
         for h in range(JT):
             (nc.vector.tensor_copy if h == 0 else nc.scalar.copy)(
                 woven[h][:].rearrange("p (c i) t -> p c t i", i=4),
-                xs_g[:, :, h * P : (h + 1) * P].rearrange("p t (c i) -> p c t i", i=4),
+                xs_g[h][:].rearrange("p t (c i) -> p c t i", i=4),
             )
         for h in range(JT):
             nc.vector.quantize_mx(
                 out=q_w[h][:].bitcast(E5), scales=q_s[h][:], in_=woven[h][:].rearrange("p c t -> p (c t)")
             )
+        g_w = [sb.tile([P, J], U32, name="g_w0", tag="woven0", align_bytes=64), sb.tile([P, J], U32, name="g_w1", align_bytes=64)]
         nc.vector.tensor_copy(g_w[0][:], xt_w[0][:].indirect(list_t[:]))
-        b2 = [sb.tile([P, N], F32, name="b2_%d" % h) for h in range(JT)]
+        nc.vector.tensor_copy(g_w[1][:], xt_w[1][:].indirect(list_t[:]))
+        b2 = sb.tile([P, JT, N], F32, name="b2", tag="xt_w1")
         for h in range(JT):
             b_ps = ps.tile([P, N], F32, name="b_ps%d" % h)
             nc.tensor.matmul_mx(
                 out=b_ps[:], lhsT=q_w[h][:].bitcast(E5), lhsT_scale=q_s[h][:],
                 rhs=wb_w[:].bitcast(E4), rhs_scale=wb_s[:], start=True, stop=True,
             )
-            nc.vector.tensor_tensor(b2[h][:], b_ps[:], bi_all[:], ALU.add)
-        nc.vector.tensor_copy(g_w[1][:], xt_w[1][:].indirect(list_t[:]))
+            nc.vector.scalar_tensor_tensor(b2[:, h, :], b_ps[:], SC, bi_all[:], ALU.mult, ALU.add)
 
         for h in range(JT):
             cols = slice(h * P, (h + 1) * P)
@@ -121,19 +121,17 @@ def tile_list_rows_othertable_largerlesssmaller_kernel(
             for z in range(PASSES):
                 nc.tensor.matmul_mx(
                     out=a_ps[:], lhsT=g_w[z][:, cols].bitcast(E5), lhsT_scale=g_s[z][:, cols],
-                    rhs=wa_w[z][:].bitcast(E5), rhs_scale=wa_s[:, z, :],
+                    rhs=wa_w[:, z, :].bitcast(E5), rhs_scale=wa_s[:, z, :],
                     start=(z == 0), stop=(z == PASSES - 1),
                 )
             sm = sb.tile([P, N], F32, name="sm%d" % h)
-            sm_sum = sb.tile([P, 1], F32, name="sm_sum%d" % h)
             shift = sb.tile([P, 1], F32, name="shift%d" % h)
             mx = sb.tile([P, N], F32, name="mx%d" % h)
             y = sb.tile([P, N], F32, name="y%d" % h)
-            nc.vector.scalar_tensor_tensor(sm[:], a_ps[:], 1.0, b2[h][:], ALU.mult, ALU.min, accum_out=sm_sum[:])
-            nc.vector.tensor_tensor(mx[:], a_ps[:], b2[h][:], ALU.max)
-            nc.scalar.activation(shift[:], sm_sum[:], ACT.Copy, scale=-2.0 / N)
+            nc.vector.scalar_tensor_tensor(sm[:], a_ps[:], SC, b2[:, h, :], ALU.mult, ALU.max, accum_out=shift[:])
+            nc.vector.scalar_tensor_tensor(mx[:], a_ps[:], SC, b2[:, h, :], ALU.mult, ALU.min)
             if h == 0:
-                nc.scalar.activation(y[:], mx[:], ACT.Identity, bias=shift[:])
+                nc.scalar.activation(y[:], mx[:], ACT.Identity, bias=shift[:], scale=1.0 / SC)
             else:
-                nc.vector.tensor_scalar(y[:], mx[:], shift[:], None, ALU.add)
+                nc.vector.tensor_scalar(y[:], mx[:], 1.0 / SC, shift[:], ALU.mult, ALU.add)
             (nc.sync if h == 0 else nc.scalar).dma_start(out[cols, :], y[:])

from contextlib import ExitStack

import concourse.mybir as mybir
from concourse.masks import make_identity

K, T, J, N, S, L = 1024, 1024, 256, 256, 512, 512
FLOPS = 2 * J * N * (K + L)

F32 = mybir.dt.float32
BF16 = mybir.dt.bfloat16
I32 = mybir.dt.int32
U32 = mybir.dt.uint32
U16 = mybir.dt.uint16
U8 = mybir.dt.uint8
E5 = mybir.dt.float8_e5m2_x4
E4 = mybir.dt.float8_e4m3fn_x4
ALU = mybir.AluOpType
ACT = mybir.ActivationFunctionType
P = 128
PASSES = K // 512
JT = J // P
SC = -2.0 / N


def tile_list_rows_othertable_largerlesssmaller_kernel(
    tc, xt_words, xt_scales, wa_words, wa_scales, xs, wb_words, wb_scales, bi, offs, offs2, out
):
    nc = tc.nc
    with ExitStack() as ctx:
        sb = ctx.enter_context(tc.tile_pool(name="sb", bufs=1))
        ps = ctx.enter_context(tc.psum_pool(name="ps", bufs=1))

        list_t = sb.tile([P, J // 16], U16, name="list_t")
        list_s = sb.tile([P, J // 16], U16, name="list_s")
        xs_sb = [sb.tile([P, 2, S], F32, name="xs_sb%d" % h, tag="xs_sb%d" % h) for h in range(2)]
        xt_w = [sb.tile([P, T], U32, name="xt_w%d" % z, tag="xt_w%d" % z) for z in range(PASSES)]
        xt_s = sb.tile([P, PASSES, T], U8, name="xt_s")
        wa_w = sb.tile([P, PASSES, N], U32, name="wa_w", align_bytes=64)
        wa_s = sb.tile([P, PASSES, N], U8, name="wa_s", align_bytes=64)
        wb_w = sb.tile([P, N], U32, name="wb_w", align_bytes=64)
        wb_s = sb.tile([P, N], U8, name="wb_s", align_bytes=64)
        bi_col = sb.tile([P, 2], F32, name="bi_col")
        ident = sb.tile([P, P], F32, name="ident")

        warm = sb.tile([P, 2], F32, name="warm")
        nc.vector.memset(xt_s[:, 0, :].bitcast(I32), 0)
        nc.gpsimd.memset(xt_s[:, 1, :].bitcast(I32), 0)
        nc.vector.memset(warm[:, 0:1], 0.0)
        nc.scalar.activation(warm[:, 1:2], warm[:, 0:1], ACT.Copy)
        nc.vector.memset(wb_s[:].bitcast(I32), 0)
        nc.vector.memset(wa_s[:].bitcast(I32), 0)

        xs_rows = xs.rearrange("(p t) s -> p t s", t=4)
        xt_s_rows = xt_scales.rearrange("z q c -> q z c").bitcast(I32)
        wa_s_rows = wa_scales.rearrange("z q c -> q z c").bitcast(I32)
        wb_s_rows = wb_scales[0].bitcast(I32)
        nc.gpsimd.dma_start(bi_col[:], bi.rearrange("o (p c) -> p (o c)", c=2))
        make_identity(nc, ident[:])
        nc.sync.dma_start(list_s[:], offs2)
        nc.sync.dma_start(list_t[:], offs)
        nc.sync.dma_start(xs_sb[0][:], xs_rows[:, 0:2, :])
        for q in range(4):
            nc.sync.dma_start(xt_s[32 * q : 32 * q + 4].bitcast(I32), xt_s_rows[4 * q : 4 * q + 4])
        nc.sync.dma_start(xs_sb[1][:], xs_rows[:, 2:4, :])
        nc.sync.dma_start(xt_w[0][:].bitcast(I32), xt_words[0].rearrange("p c r -> p (c r)").bitcast(I32))
        nc.sync.dma_start(wb_w[:].bitcast(I32), wb_words[0].rearrange("p c r -> p (c r)").bitcast(I32))
        for q in range(4):
            nc.sync.dma_start(wb_s[32 * q : 32 * q + 4].bitcast(I32), wb_s_rows[4 * q : 4 * q + 4])
        nc.sync.dma_start(xt_w[1][:].bitcast(I32), xt_words[1].rearrange("p c r -> p (c r)").bitcast(I32))
        nc.sync.dma_start(wa_w[:].bitcast(I32), wa_words.rearrange("z p c r -> p z (c r)").bitcast(I32))
        for q in range(4):
            nc.sync.dma_start(wa_s[32 * q : 32 * q + 4].bitcast(I32), wa_s_rows[4 * q : 4 * q + 4])

        g_s = [sb.tile([P, J], U8, name="g_s%d" % z, align_bytes=64) for z in range(PASSES)]
        for z in range(PASSES):
            nc.vector.tensor_copy(g_s[z][:], xt_s[:, z, :].indirect(list_t[:]))

        xs_g = [sb.tile([P, 4, P], F32, name="xs_g%d" % h) for h in range(JT)]
        for t, h in ((0, 0), (1, 0), (0, 1), (1, 1), (2, 0), (3, 0), (2, 1), (3, 1)):
            win = xs_sb[t // 2][:, t % 2, :].indirect(list_s[:, 8 * h : 8 * h + 8])
            if (t, h) == (3, 0):
                nc.vector.tensor_copy(xs_g[h][:, t, :], win)
            else:
                nc.scalar.activation(xs_g[h][:, t, :], win, ACT.Copy)

        bi_ps = ps.tile([P, 2, P], F32, name="bi_ps")
        for c in range(2):
            nc.tensor.transpose(bi_ps[:, c, :], bi_col[:, c : c + 1].to_broadcast([P, P]), ident[:])
        bi_all = sb.tile([P, N], F32, name="bi_all", tag="xs_sb1")
        nc.scalar.activation(
            bi_all[:].rearrange("q (p c) -> q p c", c=2), bi_ps[:].rearrange("q c p -> q p c"), ACT.Copy, scale=SC
        )

        woven = [sb.tile([P, P, 4], BF16, name="woven%d" % h, tag="woven%d" % h, align_bytes=64) for h in range(JT)]
        q_w = [sb.tile([P, P], U32, name="q_w%d" % h, align_bytes=64) for h in range(JT)]
        q_s = [sb.tile([P, P], U8, name="q_s%d" % h, align_bytes=64) for h in range(JT)]
        for h in range(JT):
            (nc.vector.tensor_copy if h == 0 else nc.scalar.copy)(
                woven[h][:].rearrange("p (c i) t -> p c t i", i=4),
                xs_g[h][:].rearrange("p t (c i) -> p c t i", i=4),
            )
        for h in range(JT):
            nc.vector.quantize_mx(
                out=q_w[h][:].bitcast(E5), scales=q_s[h][:], in_=woven[h][:].rearrange("p c t -> p (c t)")
            )
        g_w = [sb.tile([P, J], U32, name="g_w0", tag="woven0", align_bytes=64), sb.tile([P, J], U32, name="g_w1", align_bytes=64)]
        nc.vector.tensor_copy(g_w[0][:], xt_w[0][:].indirect(list_t[:]))
        nc.vector.tensor_copy(g_w[1][:], xt_w[1][:].indirect(list_t[:]))
        b2 = sb.tile([P, JT, N], F32, name="b2", tag="xt_w1")
        for h in range(JT):
            b_ps = ps.tile([P, N], F32, name="b_ps%d" % h)
            nc.tensor.matmul_mx(
                out=b_ps[:], lhsT=q_w[h][:].bitcast(E5), lhsT_scale=q_s[h][:],
                rhs=wb_w[:].bitcast(E4), rhs_scale=wb_s[:], start=True, stop=True,
            )
            nc.vector.scalar_tensor_tensor(b2[:, h, :], b_ps[:], SC, bi_all[:], ALU.mult, ALU.add)

        for h in range(JT):
            cols = slice(h * P, (h + 1) * P)
            a_ps = ps.tile([P, N], F32, name="a_ps%d" % h)
            for z in range(PASSES):
                nc.tensor.matmul_mx(
                    out=a_ps[:], lhsT=g_w[z][:, cols].bitcast(E5), lhsT_scale=g_s[z][:, cols],
                    rhs=wa_w[:, z, :].bitcast(E5), rhs_scale=wa_s[:, z, :],
                    start=(z == 0), stop=(z == PASSES - 1),
                )
            sm = sb.tile([P, N], F32, name="sm%d" % h)
            shift = sb.tile([P, 1], F32, name="shift%d" % h)
            mx = sb.tile([P, N], F32, name="mx%d" % h)
            y = sb.tile([P, N], F32, name="y%d" % h)
            nc.vector.scalar_tensor_tensor(sm[:], a_ps[:], SC, b2[:, h, :], ALU.mult, ALU.max, accum_out=shift[:])
            nc.vector.scalar_tensor_tensor(mx[:], a_ps[:], SC, b2[:, h, :], ALU.mult, ALU.min)
            if h == 0:
                nc.scalar.activation(y[:], mx[:], ACT.Identity, bias=shift[:], scale=1.0 / SC)
            else:
                nc.vector.tensor_scalar(y[:], mx[:], 1.0 / SC, shift[:], ALU.mult, ALU.add)
            (nc.sync if h == 0 else nc.scalar).dma_start(out[cols, :], y[:])
